import numpy as np, ml_dtypes
CORES = [37,45,53,61,69,109,117,125]
N = 8
import mx_ref
NC = 512
M = NC // N
BF = ml_dtypes.bfloat16
def cut(t, i, w=512):
    return t[:, w * i:w * i + w]
def term(a, B):
    return np.stack([mx_ref.matmul(mx_ref.quantize(cut(a, i)), B) for i in range(4)], axis=2).reshape(128, -1)
def setup_inputs(rng):
    def f(*shape):
        return mx_ref.flush((rng.standard_normal(shape, dtype=np.float32) * np.exp2(rng.integers(-2, 3, shape[:-1] + (1,)))).astype(BF))
    return {"a": f(N, 128, 4 * 512), "b": f(N, 128, 4 * NC)}
def setup_inputs_blocks(rng):
    d = setup_inputs(rng)
    for k in ("a", "b"): d[k] = mx_ref.spread(d[k], rng, 2)
    return d
def setup_inputs_wide(rng):
    d = setup_inputs(rng)
    for k in ("a", "b"): d[k] = mx_ref.flush((d[k].astype(np.float32) * np.exp2(rng.integers(-4, 5, (N, 1, 1))).astype(np.float32)).astype(BF))
    return d
def setup_inputs_lossless(rng):
    a = np.zeros((N, 128, 4 * 128, 4), np.float32)
    for r in range(N):
        k = rng.integers(0, 512, size=4 * 128)
        a[r, k // 4, np.arange(4 * 128), k % 4] = 1.0
    size = np.repeat(2.0 ** rng.integers(-4, 5, size=(1, 1, (4 * NC) // 4)), 4, axis=2)
    b = rng.integers(-1, 2, size=(N, 128, 4 * NC)) * size
    return {"a": a.reshape(N, 128, 4 * 512).astype(BF), "b": b.astype(np.float32).astype(BF)}
def reference(a, b):
    T = [term(a[r], mx_ref.quantize(b[r])) for r in range(N)]
    y = np.zeros((N, 128, 4 * M), np.float32)
    for c in range(N):
        y[c] = mx_ref.total([cut(T[r], c, 4 * M) for r in range(N)])
    return {"y": y}

from concourse.bass import DstId, RemoteDMATransfer
from concourse.mybir import dt, AluOpType, ActivationFunctionType

N = 8
PW = 64
SIM_CORES = 128
NREL = 2

SCRATCH = {
    "a_t": ("sbuf", [128, 2048], "bfloat16"),
    "b_t": ("sbuf", [128, 2048], "bfloat16"),
    "aq": ("sbuf", [128, 512], "float8_e4m3fn_x4"),
    "asc": ("sbuf", [128, 512], "uint8"),
    "bq": ("sbuf", [128, 512], "float8_e4m3fn_x4"),
    "bsc": ("sbuf", [128, 512], "uint8"),
    "ones": ("sbuf", [128, 516], "bfloat16"),
    "z": ("sbuf", [128, 516], "bfloat16"),
    "wq": ("sbuf", [128, 512], "float8_e4m3fn_x4"),
    "wsc": ("sbuf", [128, 512], "uint8"),
    "tt": ("sbuf", [128, 2048], "bfloat16"),
    "tq": ("sbuf", [128, 384], "float8_e4m3fn_x4"),
    "tsc": ("sbuf", [128, 384], "uint8"),
    "lq": ("sbuf", [128, 576], "float8_e4m3fn_x4"),
    "lsc": ("sbuf", [128, 576], "uint8"),
    "rq": ("sbuf", [128, 128], "float8_e4m3fn_x4"),
    "rsc": ("sbuf", [128, 128], "uint8"),
    "tmp": ("sbuf", [128, 256], "float32"),
    "ysb": ("sbuf", [128, 256], "float32"),
    "ps": ("psum", [128, 4096], "float32"),
}
SEMAPHORES = (["s_ones", "s_z", "s_w", "ld_b0", "ld_a0", "ld_a1", "ld_c2", "ld_c3",
               "q_b0", "q_a0", "q_a1", "q_c2", "q_c3", "e0", "e2", "e3", "t0", "t2", "t3",
               "yd", "st", "sent", "rc0", "rc1", "rs0", "rs1"]
              + ["m0_%d" % i for i in range(4)] + ["m2_%d" % i for i in range(4)] + ["m3_%d" % i for i in range(4)]
              + ["arr%d" % i for i in range(4)] + ["d%d" % i for i in range(4)] + ["c%d" % i for i in range(4)])


def _bits(m):
    return [e for e in range(16) if (m >> e) & 1]


def _pow2(n):
    k = 1
    while 2 * k <= n:
        k *= 2
    return k


def _phase(s, c):
    if c // 4 != s // 4:
        return 0
    if c // 2 != s // 2:
        return 1
    return 2


def _relays(cores, s, topo):
    me = cores[s]
    far = [c for c in cores if c != me and not topo.may_write(me, c)]
    cand = [k for k in range(SIM_CORES)
            if topo.chip(k) == topo.chip(me) and k not in cores and all(topo.may_write(k, c) for c in far)]
    cand.sort(key=lambda k: (topo.die(k) != topo.die(me), k))
    return cand[:NREL]


def _sends(cores, s, topo):
    me = cores[s]
    rel = _relays(cores, s, topo)
    rounds = []
    for b in (0, 1):
        tg = []
        j = 0
        for c in range(N):
            if c == s or min(_phase(s, c), 1) != b:
                continue
            if topo.may_write(me, cores[c]):
                tg.append((c, cores[c], None))
            else:
                tg.append((c, rel[j], j))
                j += 1
        order = sorted(tg, key=lambda t: len(_bits(topo.mask(me, t[1]))))
        used = 0
        out = []
        for n, t in enumerate(order):
            m = topo.mask(me, t[1])
            free = [e for e in _bits(m) if not (used >> e) & 1]
            peers = len([u for u in order[n:] if topo.mask(me, u[1]) == m])
            k = _pow2(len(free) // peers)
            mk = sum(1 << e for e in free[:k])
            used |= mk
            out.append((t[0], t[1], t[2], mk))
        rounds.append(out)
    return rounds


def _slots(cores, c, topo):
    items = []
    for s in range(N):
        if s == c:
            items.append((1.0, s))
        else:
            hops = 1 if topo.may_write(cores[s], cores[c]) else 2
            items.append((0.5 * _phase(s, c) + 2.0 * hops, s))
    items.sort()
    order = [s for _, s in items]
    pairs = [order[2 * k:2 * k + 2] for k in range(4)]
    slot = {}
    wins = []
    w = 0
    for p in pairs:
        if c in p:
            slot[p[0] if p[1] == c else p[1]] = 6
            slot[c] = 7
            wins.append(3)
        else:
            slot[p[0]] = 2 * w
            slot[p[1]] = 2 * w + 1
            wins.append(w)
            w += 1
    return slot, pairs, wins


def _last_engines(cores, s, c, topo):
    for rnd in _sends(cores, s, topo):
        for (o, tgt, j, mk) in rnd:
            if o == c:
                if j is None:
                    return len(_bits(mk))
                return len(_bits(topo.mask(tgt, cores[c])))
    return 0


def _cols(t, lo, n):
    return t[:, lo:lo + n]


def _helper(g, core, T, topo, cores):
    for s in range(N):
        rel = _relays(cores, s, topo)
        if core not in rel:
            continue
        j = rel.index(core)
        total = 0
        for b, rnd in enumerate(_sends(cores, s, topo)):
            for (o, tgt, jj, mk) in rnd:
                if jj != j:
                    continue
                k_in = len(_bits(mk))
                dst = cores[o]
                rid, pid, _ = topo.addr(dst)
                m = topo.mask(core, dst)
                slot = _slots(cores, o, topo)[0][s]
                sem = T.sem["arr%d" % (slot // 2)]
                g.wait_ge(T.sem["rc%d" % b], k_in)
                g.remote_dma(_cols(T.lq, PW * slot, PW).bitcast(dt.uint8), _cols(T.rq, PW * b, PW).bitcast(dt.uint8),
                             sem, T.sem.sent, pid, rid, m)
                g.wait_ge(T.sem["rs%d" % b], k_in)
                g.remote_dma(_cols(T.lsc, PW * slot, PW), _cols(T.rsc, PW * b, PW), sem, T.sem.sent, pid, rid, m)
                total += 2 * len(_bits(m))
        if total:
            g.wait_ge(T.sem.sent, total)


def rank_program(g, core, T, topo):
    cores = [int(c) for c in T.cores]
    r = T.rank_of(core)
    if r is None:
        _helper(g, core, T, topo, cores)
        return
    S = T.sem
    q = r // 2
    h = q // 2
    w0 = 256 * (1 - h)
    w2 = 128 * (q ^ 1)
    w3 = 128 * q
    V, P, A, Y = g.vector, g.tensor, g.scalar, g.sync
    Copy = ActivationFunctionType.Copy

    Y.dma_start(_cols(T.b_t, 4 * w0, 1024), _cols(T.b, 4 * w0, 1024)).then_inc(S.ld_b0, 16)
    A.dma_start(_cols(T.a_t, 0, 1024), _cols(T.a, 0, 1024)).then_inc(S.ld_a0, 16)
    Y.dma_start(_cols(T.a_t, 1024, 1024), _cols(T.a, 1024, 1024)).then_inc(S.ld_a1, 16)
    A.dma_start(_cols(T.b_t, 4 * w2, 512), _cols(T.b, 4 * w2, 512)).then_inc(S.ld_c2, 16)
    Y.dma_start(_cols(T.b_t, 4 * w3, 512), _cols(T.b, 4 * w3, 512)).then_inc(S.ld_c3, 16)

    V.memset(T.ones[:], 1.0).then_inc(S.s_ones, 1)
    g.wait_ge(S.s_ones, 1)
    g.affine_select(T.z[:], T.ones[:], [[-1, 516]], AluOpType.is_equal, 0.0, 3, 4).then_inc(S.s_z, 1)
    V.wait_ge(S.s_z, 1)
    for i in range(4):
        V.quantize_mx(_cols(T.wq, 128 * i, 128), _cols(T.wsc, 128 * i, 128), _cols(T.z, 3 - i, 512)).then_inc(S.s_w, 1)

    def product(i, bank, w, n, sem):
        P.matmul_mx(_cols(T.ps, 512 * bank, n), _cols(T.aq, 128 * i, 128), _cols(T.asc, 128 * i, 128),
                    _cols(T.bq, w, n), _cols(T.bsc, w, n), True, True).then_inc(sem, 1)

    P.wait_ge(S.q_b0, 1)
    P.wait_ge(S.q_a0, 1)
    product(0, 0, w0, 256, S.m0_0)
    product(1, 1, w0, 256, S.m0_1)
    P.wait_ge(S.q_a1, 1)
    product(2, 2, w0, 256, S.m0_2)
    product(3, 3, w0, 256, S.m0_3)
    P.wait_ge(S.q_c2, 1)
    for i in range(4):
        product(i, 4 + i, w2, 128, S["m2_%d" % i])
    P.wait_ge(S.q_c3, 1)
    P.wait_ge(S.e0, 4)
    for i in range(4):
        product(i, i, w3, 128, S["m3_%d" % i])

    def evac(eng, i, which):
        def put(out, in_, sem):
            if eng is A:
                A.activation(out, in_, Copy).then_inc(sem, 1)
            else:
                V.tensor_copy(out, in_).then_inc(sem, 1)
        if which == 0:
            eng.wait_ge(S["m0_%d" % i], 1)
            put(T.tt[:, i:1024:4], _cols(T.ps, 512 * i, 256), S.e0)
        elif which == 2:
            eng.wait_ge(S["m2_%d" % i], 1)
            put(T.tt[:, 1024 + i:1536:4], _cols(T.ps, 512 * (4 + i), 128), S.e2)
        else:
            eng.wait_ge(S["m3_%d" % i], 1)
            own = r % 2
            put(T.tt[:, 1536 + i:1792:4], _cols(T.ps, 512 * i + PW * own, PW), S.e3)
            put(T.tt[:, 1792 + i:2048:4], _cols(T.ps, 512 * i + PW * (1 - own), PW), S.e3)

    for which in (0, 2, 3):
        evac(A, 0, which)
        evac(A, 2, which)

    V.wait_ge(S.ld_b0, 16)
    V.quantize_mx(_cols(T.bq, w0, 256), _cols(T.bsc, w0, 256), _cols(T.b_t, 4 * w0, 1024)).then_inc(S.q_b0, 1)
    V.wait_ge(S.ld_a0, 16)
    V.quantize_mx(_cols(T.aq, 0, 256), _cols(T.asc, 0, 256), _cols(T.a_t, 0, 1024)).then_inc(S.q_a0, 1)
    V.wait_ge(S.ld_a1, 16)
    V.quantize_mx(_cols(T.aq, 256, 256), _cols(T.asc, 256, 256), _cols(T.a_t, 1024, 1024)).then_inc(S.q_a1, 1)
    evac(V, 1, 0)
    V.wait_ge(S.ld_c2, 16)
    V.quantize_mx(_cols(T.bq, w2, 128), _cols(T.bsc, w2, 128), _cols(T.b_t, 4 * w2, 512)).then_inc(S.q_c2, 1)
    evac(V, 3, 0)
    V.wait_ge(S.e0, 4)
    V.quantize_mx(_cols(T.tq, 0, 256), _cols(T.tsc, 0, 256), _cols(T.tt, 0, 1024)).then_inc(S.t0, 1)
    V.wait_ge(S.ld_c3, 16)
    V.quantize_mx(_cols(T.bq, w3, 128), _cols(T.bsc, w3, 128), _cols(T.b_t, 4 * w3, 512)).then_inc(S.q_c3, 1)
    evac(V, 1, 2)
    evac(V, 3, 2)
    V.wait_ge(S.e2, 4)
    V.quantize_mx(_cols(T.tq, 256, 128), _cols(T.tsc, 256, 128), _cols(T.tt, 1024, 512)).then_inc(S.t2, 1)
    evac(V, 1, 3)
    evac(V, 3, 3)
    V.wait_ge(S.e3, 8)
    V.quantize_mx(_cols(T.lq, 7 * PW, 128), _cols(T.lsc, 7 * PW, 128), _cols(T.tt, 1536, 512)).then_inc(S.t3, 1)

    def source(c):
        ph = _phase(r, c)
        if ph == 0:
            return T.tq, T.tsc, PW * (c % 4)
        if ph == 1:
            return T.tq, T.tsc, 256 + PW * (c % 2)
        return T.lq, T.lsc, 8 * PW

    sent = 0
    for b, rnd in enumerate(_sends(cores, r, topo)):
        if b == 0:
            g.wait_ge(S.t0, 1)
        else:
            g.wait_ge(S.t2, 1)
            g.wait_ge(S.t3, 1)
        codes, planes = [], []
        for (o, tgt, j, mk) in rnd:
            cq, cs, lo = source(o)
            rid, pid, _ = topo.addr(tgt)
            to = [DstId(rid=rid, pnc=pid)]
            if j is None:
                slot = _slots(cores, o, topo)[0][r]
                sem_c = sem_s = S["arr%d" % (slot // 2)]
                dq, ds, dlo = T.lq, T.lsc, PW * slot
            else:
                sem_c, sem_s = S["rc%d" % b], S["rs%d" % b]
                dq, ds, dlo = T.rq, T.rsc, PW * b
            codes.append(RemoteDMATransfer(dst_ids=to, dma_engine_mask=mk, remote_sem=sem_c,
                                           src=_cols(cq, lo, PW).bitcast(dt.uint8),
                                           dst=_cols(dq, dlo, PW).bitcast(dt.uint8)))
            planes.append(RemoteDMATransfer(dst_ids=to, dma_engine_mask=mk, remote_sem=sem_s,
                                            src=_cols(cs, lo, PW), dst=_cols(ds, dlo, PW)))
            sent += 2 * len(_bits(mk))
        g.remote_dma_fused(codes, local_sem=S.sent)
        g.remote_dma_fused(planes, local_sem=S.sent)

    slot, pairs, wins = _slots(cores, r, topo)
    P.wait_ge(S.s_w, 4)
    P.wait_ge(S.e2, 4)
    for k, (pair, win) in enumerate(zip(pairs, wins)):
        need = sum(2 * _last_engines(cores, s, r, topo) for s in pair if s != r)
        P.wait_ge(S["arr%d" % win], need)
        if r in pair:
            P.wait_ge(S.t3, 1)
        for i in range(4):
            mm = P.matmul_mx(_cols(T.ps, 512 * (4 + i), 128), _cols(T.wq, 128 * i, 128), _cols(T.wsc, 128 * i, 128),
                             _cols(T.lq, 128 * win, 128), _cols(T.lsc, 128 * win, 128), k == 0, k == 3)
            if k == 3:
                mm.then_inc(S["d%d" % i], 1)

    for i in range(4):
        A.wait_ge(S["d%d" % i], 1)
        A.activation(_cols(T.tmp, PW * i, PW), _cols(T.ps, 512 * (4 + i) + PW, PW), Copy).then_inc(S["c%d" % i], 1)
        V.wait_ge(S["c%d" % i], 1)
        V.tensor_tensor(T.ysb[:, i:256:4], _cols(T.ps, 512 * (4 + i), PW), _cols(T.tmp, PW * i, PW),
                        AluOpType.add).then_inc(S.yd, 1)
    Y.wait_ge(S.yd, 4)
    Y.dma_start(T.y[:], T.ysb[:]).then_inc(S.st, 16)
    Y.wait_ge(S.st, 16)
    g.wait_ge(S.sent, sent)
